import numpy as np
import ml_dtypes


def mxq(x, axis, fmt="e4m3"):
    dtype, down = {"e4m3": (ml_dtypes.float8_e4m3fn, 7), "e5m2": (ml_dtypes.float8_e5m2, 14)}[fmt]
    v = np.moveaxis(np.asarray(x, np.float32).astype(ml_dtypes.bfloat16).astype(np.float64), axis, -1)
    blocks = v.reshape(v.shape[:-1] + (-1, 32))
    amax = np.abs(blocks).max(-1, keepdims=True)
    byte = np.maximum(np.where(amax > 0, np.frexp(amax)[1] - 1 + 127, 0) - down, 1)
    scale = np.exp2(byte - 127.0)
    codes = (blocks / scale).astype(np.float32).astype(dtype).astype(np.float64)
    return np.moveaxis((codes * scale).reshape(v.shape), -1, axis)


WIDE = False


def mx_kscale(k):
    if not WIDE:
        return np.ones(k)
    levels = np.array([10, -10, 5, -5, 0])
    if k % 512:
        return np.exp2(np.random.permutation(np.resize(levels, k // 32))).repeat(32)
    a = np.empty((k // 512, 16))
    for p in range(k // 512):
        a[p, :8] = np.random.permutation(np.resize(levels, 8))
        for g in range(8):
            far = levels[np.abs(levels - a[p, g]) >= 10]
            a[p, g + 8] = far[np.random.randint(len(far))]
    return np.exp2(a.ravel()).repeat(32)


def f64(x):
    return np.asarray(x).astype(np.float64)


def striped(idx):
    return np.tile(idx.reshape(-1, 16).T, (8, 1)).astype(np.uint16)


def unstriped(offs):
    return offs[:16].T.reshape(-1).astype(np.int64)


def striped8(idx):
    return np.concatenate([x.reshape(-1, 16).T for x in idx]).astype(np.uint16)


def runs(offs, k):
    lists = np.stack([offs[16 * r : 16 * r + 16].T.reshape(-1) for r in range(8)]).astype(np.int64)
    return lists[np.arange(k) % 512 // 64]


def pack_weight(w):
    k, n = w.shape
    w = f64(np.asarray(w, np.float32).astype(ml_dtypes.bfloat16)).reshape(k // 32, 32, n)
    amax = np.abs(w).max(1)
    byte = np.clip(np.where(amax > 0, np.frexp(amax)[1] - 1 + 127 - 7, 1), 1, 254)
    scaled = (w * np.exp2(127.0 - byte)[:, None, :]).reshape(k, n).astype(np.float32)
    words = np.ascontiguousarray(scaled.reshape(k // 512, 128, 4, n).transpose(0, 1, 3, 2)).astype(ml_dtypes.float8_e4m3fn).view(np.uint8)
    return words, np.ascontiguousarray(byte.astype(np.uint8).reshape(k // 512, 16, n))


def unpack_weight(words, scales):
    g, p, n, _ = words.shape
    vals = np.ascontiguousarray(words).view(ml_dtypes.float8_e4m3fn).astype(np.float64) * np.repeat(np.exp2(scales.astype(np.float64) - 127.0), 8, axis=1)[..., None]
    return vals.transpose(0, 1, 3, 2).reshape(g * 512, n)


def sigmoid(v):
    return 1.0 / (1.0 + np.exp(-np.maximum(v, -700.0)))

def planes(y):
    n, m = y.shape
    v = y.astype(np.float32).astype(ml_dtypes.bfloat16).astype(np.float64).reshape(n // 32, 32, m)
    top = np.abs(v).max(1)
    byte = np.clip(np.where(top > 0, np.frexp(top)[1] - 1 + 127 - 7, 1), 1, 254)
    codes = (v * np.exp2(127.0 - byte)[:, None, :]).reshape(n, m).astype(np.float32).astype(ml_dtypes.float8_e4m3fn).view(np.uint8)
    words = codes.reshape(n // 512, 128, 4, m).transpose(0, 1, 3, 2)
    return np.ascontiguousarray(words), np.ascontiguousarray(byte.astype(np.uint8).reshape(n // 512, 16, m))


K, T, S, N, H, U = 512, 2048, 512, 512, 512, 1024


def setup_inputs():
    n = np.random.standard_normal
    s = mx_kscale(K)[:, None]
    u = mx_kscale(H)
    packed_xT = pack_weight(n((K, T)) * s)
    packed_w1 = pack_weight(n((K, H)) / np.sqrt(K) / s)
    packed_w2 = pack_weight(n((K, H)) / np.sqrt(K) / s)
    packed_w3 = pack_weight(n((H, N)) / np.sqrt(H) / u[:, None])
    return {
        "x_words": packed_xT[0],
        "x_scales": packed_xT[1],
        "w1_words": packed_w1[0],
        "w1_scales": packed_w1[1],
        "w2_words": packed_w2[0],
        "w2_scales": packed_w2[1],
        "tel": n((H, S)).astype(np.float32),
        "gn": (np.random.uniform(0.5, 1.5, (H, 1)) * u[:, None]).astype(np.float32),
        "w3_words": packed_w3[0],
        "w3_scales": packed_w3[1],
        "mem": n((N, U)).astype(np.float32),
        "offs": striped(np.random.permutation(T)[:S]),
        "two": striped(np.random.permutation(T)[:S]),
        "in1": striped8(np.stack([np.random.permutation(S) for _ in range(8)])),
        "in2": striped8(np.stack([np.random.permutation(S) for _ in range(8)])),
        "slot": striped8(np.stack([np.random.permutation(U)[:S] for _ in range(8)])),
    }


def reference(x_words, x_scales, w1_words, w1_scales, w2_words, w2_scales, tel, gn, w3_words, w3_scales, mem, offs, two, in1, in2, slot):
    xq = unpack_weight(x_words, x_scales)[:, unstriped(offs)]
    y = unpack_weight(w1_words, w1_scales).T @ xq
    x_two = unpack_weight(x_words, x_scales)[:, unstriped(two)]
    c = sigmoid(unpack_weight(w2_words, w2_scales).T @ x_two)
    sh = y / (c + 0.25)
    z = f64(gn) * (0.5 * (sh[np.arange(H)[:, None], runs(in1, H)] + sh[np.arange(H)[:, None], runs(in2, H)]) + 0.5 * f64(tel))
    h = unpack_weight(w3_words, w3_scales).T @ mxq(z, 0, "e4m3")
    out = f64(mem).copy()
    out[np.arange(N)[:, None], runs(slot, N)] = h
    return (out,) + planes(out)

@@ -1,0 +1,262 @@
+import math
+from contextlib import ExitStack
+
+import concourse.mybir as mybir
+
+F32 = mybir.dt.float32
+BF16 = mybir.dt.bfloat16
+I32 = mybir.dt.int32
+U32 = mybir.dt.uint32
+U16 = mybir.dt.uint16
+U8 = mybir.dt.uint8
+FP8X4 = mybir.dt.float8_e4m3fn_x4
+ACT = mybir.ActivationFunctionType
+ALU = mybir.AluOpType
+
+P = 128
+PACK = 4
+T, S, U = 2048, 512, 1024
+FEATURES = P * PACK
+CHUNKS = ((0, 256), (256, 384), (384, 512))
+HALF = U // 2
+
+FLOPS = 3 * 2 * FEATURES * FEATURES * S
+
+
+def offsets(lists, lo, hi):
+    return lists[:, lo // 16 : hi // 16]
+
+
+def words_view(words):
+    return words[0].rearrange("p n t -> p (n t)").bitcast(I32)
+
+
+def load_scale_rows(queues, tile, first, scales):
+    for q, queue in enumerate(queues):
+        row = 32 * q + first
+        queue.dma_start(out=tile[row : row + 4, :].bitcast(I32), in_=scales[0, 4 * q : 4 * q + 4, :].bitcast(I32))
+
+
+def deal_columns(nc, dealt, raw, run):
+    nc.vector.tensor_copy(
+        out=dealt.rearrange("p (t c i) -> p c t i", t=PACK, i=run),
+        in_=raw.rearrange("p (c i t) -> p c t i", t=PACK, i=run),
+    )
+
+
+def tile_picked_rankstep_none_po_kernel(
+    tc, x_words, x_scales, w1_words, w1_scales, w2_words, w2_scales, tel, gn, w3_words, w3_scales, mem,
+    offs, two, in1, in2, slot, out_0, out_1, out_2,
+):
+    nc = tc.nc
+    with ExitStack() as ctx:
+        keep = ctx.enter_context(tc.tile_pool(name="keep", bufs=1))
+        psum = ctx.enter_context(tc.psum_pool(name="psum", bufs=1))
+
+        def sbuf(name, shape, dtype, tag=None):
+            return keep.tile(shape, dtype, name=name, tag=tag or name, align_bytes=64)
+
+        def load_list(name, lists):
+            tile = keep.tile([P, S // 16], U16, name=name)
+            nc.sync.dma_start(tile[:], lists)
+            return tile
+
+        def load_words(name, words, width):
+            tile = sbuf(name, [P, width], U32)
+            nc.sync.dma_start(out=tile[:].bitcast(I32), in_=words_view(words))
+            return tile
+
+        x_scale_table = sbuf("x_scale_table", [P, T], U8)
+        w12_scale_raw = sbuf("w12_scale_raw", [P, FEATURES], U8)
+        w3_scale_raw = sbuf("w3_scale_raw", [P, FEATURES], U8)
+        nc.vector.memset(w12_scale_raw[:].bitcast(I32), 0)
+        nc.vector.memset(w3_scale_raw[:].bitcast(I32), 0)
+
+        two_list = load_list("two_list", two)
+        for q in range(4):
+            nc.sync.dma_start(
+                out=x_scale_table[32 * q : 32 * q + 32, :].bitcast(I32),
+                in_=x_scales[0, 4 * q : 4 * q + 4, :].bitcast(I32).unsqueeze(0).to_broadcast([8, 4, T // 4]),
+            )
+        offs_list = load_list("offs_list", offs)
+        w2_raw = load_words("w2_raw", w2_words, FEATURES)
+        x_word_table = load_words("x_word_table", x_words, T)
+        load_scale_rows([nc.sync] * 4, w12_scale_raw, 0, w2_scales)
+        load_scale_rows([nc.sync] * 2 + [nc.gpsimd] * 2, w12_scale_raw, 4, w1_scales)
+        w1_raw = load_words("w1_raw", w1_words, FEATURES)
+        gain = sbuf("gain", [P, PACK], F32)
+        nc.gpsimd.dma_start(out=gain[:], in_=gn.rearrange("(p t) o -> p (t o)", t=PACK))
+        in1_list = load_list("in1_list", in1)
+        tel_rows = tel.rearrange("(p t) j -> p t j", t=PACK)
+        tel_raw = [sbuf(f"tel_raw{t}", [P, S], F32) for t in range(PACK)]
+        for t in range(PACK):
+            nc.sync.dma_start(out=tel_raw[t][:], in_=tel_rows[:, t, :])
+            if t == 0:
+                in2_list = load_list("in2_list", in2)
+                w3_raw = load_words("w3_raw", w3_words, FEATURES)
+                load_scale_rows([nc.sync] * 4, w3_scale_raw, 0, w3_scales)
+        slot_list = load_list("slot_list", slot)
+        mem_rows = mem.rearrange("(p t) c -> p t c", t=PACK)
+        page = [sbuf(f"page{t}", [P, U], F32) for t in range(PACK)]
+        for t in range(PACK):
+            nc.sync.dma_start(out=page[t][:], in_=mem_rows[:, t, :])
+
+        factor_scale = sbuf("factor_scale", [P, PACK], F32)
+        factor_bias = sbuf("factor_bias", [P, PACK], F32)
+        tel_scale = sbuf("tel_scale", [P, PACK], F32)
+        nc.gpsimd.tensor_scalar(factor_scale[:], gain[:], 1.6, 0.0, ALU.mult, ALU.add)
+        nc.gpsimd.tensor_scalar(factor_bias[:], gain[:], 0.4, 0.0, ALU.mult, ALU.add)
+        nc.gpsimd.tensor_scalar(tel_scale[:], gain[:], 0.5, 0.0, ALU.mult, ALU.add)
+
+        two_scales = sbuf("two_scales", [P, S], U8)
+        offs_scales = sbuf("offs_scales", [P, S], U8)
+        two_words = sbuf("two_words", [P, S], U32)
+        w12_scale = sbuf("w12_scale", [P, FEATURES], U8)
+        w3_scale = sbuf("w3_scale", [P, FEATURES], U8)
+        w1_dealt = sbuf("w1_dealt", [P, FEATURES], U32)
+        w2_dealt = sbuf("w2_dealt", [P, FEATURES], U32)
+        w3_dealt = sbuf("w3_dealt", [P, FEATURES], U32)
+        nc.vector.tensor_copy(two_scales[:], x_scale_table[:].indirect(two_list[:]))
+        nc.vector.tensor_copy(offs_scales[:], x_scale_table[:].indirect(offs_list[:]))
+        deal_columns(nc, w2_dealt[:].bitcast(I32), w2_raw[:].bitcast(I32), 4)
+        deal_columns(nc, w12_scale[:], w12_scale_raw[:], 16)
+        nc.vector.tensor_copy(two_words[:], x_word_table[:].indirect(two_list[:]))
+        offs_words = sbuf("offs_words", [P, S], U32, tag="w12_scale_raw")
+        nc.vector.tensor_copy(offs_words[:], x_word_table[:].indirect(offs_list[:]))
+        deal_columns(nc, w1_dealt[:].bitcast(I32), w1_raw[:].bitcast(I32), 4)
+        deal_columns(nc, w3_dealt[:].bitcast(I32), w3_raw[:].bitcast(I32), 4)
+        deal_columns(nc, w3_scale[:], w3_scale_raw[:], 16)
+
+        def product(out, weights, weight_scales, first, t, moving, moving_scales):
+            cols = slice(t * P, (t + 1) * P)
+            nc.tensor.matmul_mx(
+                out=out,
+                lhsT=weights[:, cols].bitcast(FP8X4),
+                lhsT_scale=weight_scales[first:P, cols],
+                rhs=moving.bitcast(FP8X4),
+                rhs_scale=moving_scales,
+                start=True,
+                stop=True,
+            )
+
+        degree = [psum.tile([P, S], F32, name=f"degree{t}", tag=f"bank{t}") for t in range(PACK)]
+        rank = [psum.tile([P, S], F32, name=f"rank{t}", tag=f"bank{PACK + t}") for t in range(PACK)]
+        product(degree[0][:], w2_dealt, w12_scale, 0, 0, two_words[:], two_scales[:])
+        for t in range(PACK):
+            if t + 1 < PACK:
+                product(degree[t + 1][:], w2_dealt, w12_scale, 0, t + 1, two_words[:], two_scales[:])
+            product(rank[t][:], w1_dealt, w12_scale, 4, t, offs_words[:], offs_scales[:])
+
+        share = [sbuf(f"share{t}", [P, S], F32) for t in range(PACK)]
+        jump = [sbuf(f"jump{t}", [P, S], F32) for t in range(PACK)]
+        gate = [sbuf(f"gate{t}", [P, S], F32) for t in range(PACK)]
+        factor = [sbuf(f"factor{t}", [P, S], F32) for t in range(PACK)]
+        for t in range(PACK):
+            nc.scalar.activation(gate[t][:], degree[t][:], ACT.Sigmoid, bias=-math.log(5.0), scale=-1.0)
+            nc.scalar.activation(
+                factor[t][:], gate[t][:], ACT.Identity, bias=factor_bias[:, t : t + 1], scale=factor_scale[:, t : t + 1]
+            )
+            nc.scalar.activation(jump[t][:], tel_raw[t][:], ACT.Copy, scale=tel_scale[:, t : t + 1])
+
+        result = sbuf("result", [P, PACK, S], F32)
+        partial, z, z_grouped, acc = {}, {}, {}, {}
+
+        def first_gather(n, t, tag=None):
+            lo, hi = CHUNKS[n]
+            partial[n, t] = sbuf(f"partial{n}_{t}", [P, hi - lo], F32, tag=tag)
+            nc.vector.tensor_tensor(
+                partial[n, t][:], share[t][:].indirect(offsets(in1_list, lo, hi)), jump[t][:, lo:hi], ALU.add
+            )
+
+        def second_gather(n, t):
+            lo, hi = CHUNKS[n]
+            if t == 0:
+                z[n] = sbuf(f"z{n}", [P, PACK, hi - lo], F32)
+            nc.vector.tensor_tensor(
+                z[n][:, t, :], share[t][:].indirect(offsets(in2_list, lo, hi)), partial[n, t][:], ALU.add
+            )
+
+        def group_z(n):
+            lo, hi = CHUNKS[n]
+            z_grouped[n] = sbuf(f"z_grouped{n}", [P, hi - lo, PACK], BF16)
+            nc.scalar.copy(
+                z_grouped[n][:].rearrange("p (c i) t -> p c t i", i=4),
+                z[n][:].rearrange("p t (c i) -> p c t i", i=4),
+            )
+
+        def last_product(n, banks):
+            lo, hi = CHUNKS[n]
+            z_words = sbuf(f"z_words{n}", [P, hi - lo], U32)
+            z_scales = sbuf(f"z_scales{n}", [P, hi - lo], U8)
+            nc.vector.quantize_mx(
+                out=z_words[:].bitcast(FP8X4), scales=z_scales[:], in_=z_grouped[n][:].rearrange("p c t -> p (c t)")
+            )
+            per_bank = PACK // len(banks)
+            for b, bank in enumerate(banks):
+                tile = psum.tile([P, per_bank, hi - lo], F32, name=f"acc{n}_{b}", tag=f"bank{bank}")
+                for j in range(per_bank):
+                    product(tile[:, j, :], w3_dealt, w3_scale, 0, b * per_bank + j, z_words[:], z_scales[:])
+                acc[n, b] = tile
+
+        def scatter(t, lo, hi, values):
+            nc.vector.tensor_copy(page[t][:].indirect(offsets(slot_list, lo, hi)), values)
+
+        (a_lo, a_hi), (b_lo, b_hi), (c_lo, c_hi) = CHUNKS
+        steps = [(n, t) for n in range(len(CHUNKS)) for t in range(PACK)]
+        nc.vector.tensor_tensor(share[0][:], rank[0][:], factor[0][:], ALU.mult)
+        for i, (n, t) in enumerate(steps):
+            if (n, t) == (2, 0):
+                last_product(0, (0, 1))
+                nc.scalar.copy(result[:, 1, a_lo:a_hi], acc[0, 0][:, 1, :])
+                nc.scalar.copy(result[:, 2:4, a_lo:a_hi], acc[0, 1][:])
+            if (n, t) == (2, 3):
+                last_product(1, (2,))
+                nc.scalar.copy(result[:, 1:4, b_lo:b_hi], acc[1, 0][:, 1:4, :])
+            first_gather(n, t, {(2, 0): "z_grouped0", (2, 3): "z_grouped1"}.get((n, t)))
+            if i + 1 < PACK:
+                nc.vector.tensor_tensor(share[i + 1][:], rank[i + 1][:], factor[i + 1][:], ALU.mult)
+            if i > 0:
+                second_gather(*steps[i - 1])
+                if t == 0:
+                    group_z(n - 1)
+        first_a = sbuf("first_a", [P, a_hi - a_lo], F32, tag="jump3")
+        nc.scalar.copy(first_a[:], acc[0, 0][:, 0, :])
+        second_gather(*steps[-1])
+        group_z(2)
+        first_b = sbuf("first_b", [P, b_hi - b_lo], F32, tag="z2")
+        nc.scalar.copy(first_b[:], acc[1, 0][:, 0, :])
+        scatter(0, a_lo, a_hi, first_a[:])
+        last_product(2, (3,))
+        nc.scalar.copy(result[:, 0, c_lo:c_hi], acc[2, 0][:, 0, :])
+        nc.scalar.copy(result[:, 1:4, c_lo:c_hi], acc[2, 0][:, 1:4, :])
+        scatter(0, b_lo, b_hi, first_b[:])
+        scatter(0, c_lo, c_hi, result[:, 0, c_lo:c_hi])
+
+        out_rows = out_0.rearrange("(p t) c -> p t c", t=PACK)
+        grouped = [sbuf(f"grouped{h}", [P, HALF, PACK], BF16) for h in range(2)]
+        for t in range(PACK):
+            if t > 0:
+                scatter(t, 0, S, result[:, t, :])
+            nc.sync.dma_start(out=out_rows[:, t, :], in_=page[t][:])
+            for h in range(2):
+                cols = slice(h * HALF, (h + 1) * HALF)
+                if t == PACK - 1 and h == 0:
+                    nc.vector.tensor_copy(grouped[h][:, :, t], page[t][:, cols])
+                elif t == PACK - 2 and h == 0:
+                    nc.scalar.copy(grouped[h][:, :, t:], page[t][:, cols].unsqueeze(2).to_broadcast([P, HALF, 2]))
+                else:
+                    nc.scalar.copy(grouped[h][:, :, t], page[t][:, cols])
+
+        out_scales = sbuf("out_scales", [P, U], U8)
+        for h in range(2):
+            cols = slice(h * HALF, (h + 1) * HALF)
+            out_words = sbuf(f"out_words{h}", [P, HALF], U32)
+            nc.vector.quantize_mx(
+                out=out_words[:].bitcast(FP8X4), scales=out_scales[:, cols], in_=grouped[h][:].rearrange("p c t -> p (c t)")
+            )
+            nc.sync.dma_start(out=words_view(out_1)[:, cols], in_=out_words[:].bitcast(I32))
+        for q in range(4):
+            queue = nc.sync if q % 2 == 0 else nc.scalar
+            queue.dma_start(
+                out=out_2[0, 4 * q : 4 * q + 4, :].bitcast(I32), in_=out_scales[32 * q : 32 * q + 4, :].bitcast(I32)
+            )

@@ -18,7 +18,7 @@ PACK = 4
 T, S, U = 2048, 512, 1024
 FEATURES = P * PACK
 CHUNKS = ((0, 256), (256, 384), (384, 512))
-HALF = U // 2
+OUT_PARTS = ((0, 256), (256, 512), (512, 768), (768, 1024))
 
 FLOPS = 3 * 2 * FEATURES * FEATURES * S
 
@@ -74,7 +74,7 @@ def tile_picked_rankstep_none_po_kernel(
 
         two_list = load_list("two_list", two)
         for q in range(4):
-            nc.sync.dma_start(
+            (nc.sync if q < 2 else nc.scalar).dma_start(
                 out=x_scale_table[32 * q : 32 * q + 32, :].bitcast(I32),
                 in_=x_scales[0, 4 * q : 4 * q + 4, :].bitcast(I32).unsqueeze(0).to_broadcast([8, 4, T // 4]),
             )
@@ -86,6 +86,8 @@ def tile_picked_rankstep_none_po_kernel(
         w1_raw = load_words("w1_raw", w1_words, FEATURES)
         gain = sbuf("gain", [P, PACK], F32)
         nc.gpsimd.dma_start(out=gain[:], in_=gn.rearrange("(p t) o -> p (t o)", t=PACK))
+        w3_raw = load_words("w3_raw", w3_words, FEATURES)
+        load_scale_rows([nc.sync] * 4, w3_scale_raw, 0, w3_scales)
         in1_list = load_list("in1_list", in1)
         tel_rows = tel.rearrange("(p t) j -> p t j", t=PACK)
         tel_raw = [sbuf(f"tel_raw{t}", [P, S], F32) for t in range(PACK)]
@@ -93,8 +95,6 @@ def tile_picked_rankstep_none_po_kernel(
             nc.sync.dma_start(out=tel_raw[t][:], in_=tel_rows[:, t, :])
             if t == 0:
                 in2_list = load_list("in2_list", in2)
-                w3_raw = load_words("w3_raw", w3_words, FEATURES)
-                load_scale_rows([nc.sync] * 4, w3_scale_raw, 0, w3_scales)
         slot_list = load_list("slot_list", slot)
         mem_rows = mem.rearrange("(p t) c -> p t c", t=PACK)
         page = [sbuf(f"page{t}", [P, U], F32) for t in range(PACK)]
@@ -119,8 +119,8 @@ def tile_picked_rankstep_none_po_kernel(
         nc.vector.tensor_copy(two_scales[:], x_scale_table[:].indirect(two_list[:]))
         nc.vector.tensor_copy(offs_scales[:], x_scale_table[:].indirect(offs_list[:]))
         deal_columns(nc, w2_dealt[:].bitcast(I32), w2_raw[:].bitcast(I32), 4)
-        deal_columns(nc, w12_scale[:], w12_scale_raw[:], 16)
         nc.vector.tensor_copy(two_words[:], x_word_table[:].indirect(two_list[:]))
+        deal_columns(nc, w12_scale[:], w12_scale_raw[:], 16)
         offs_words = sbuf("offs_words", [P, S], U32, tag="w12_scale_raw")
         nc.vector.tensor_copy(offs_words[:], x_word_table[:].indirect(offs_list[:]))
         deal_columns(nc, w1_dealt[:].bitcast(I32), w1_raw[:].bitcast(I32), 4)
@@ -158,7 +158,6 @@ def tile_picked_rankstep_none_po_kernel(
             )
             nc.scalar.activation(jump[t][:], tel_raw[t][:], ACT.Copy, scale=tel_scale[:, t : t + 1])
 
-        result = sbuf("result", [P, PACK, S], F32)
         partial, z, z_grouped, acc = {}, {}, {}, {}
 
         def first_gather(n, t, tag=None):
@@ -191,12 +190,11 @@ def tile_picked_rankstep_none_po_kernel(
             nc.vector.quantize_mx(
                 out=z_words[:].bitcast(FP8X4), scales=z_scales[:], in_=z_grouped[n][:].rearrange("p c t -> p (c t)")
             )
-            per_bank = PACK // len(banks)
-            for b, bank in enumerate(banks):
-                tile = psum.tile([P, per_bank, hi - lo], F32, name=f"acc{n}_{b}", tag=f"bank{bank}")
-                for j in range(per_bank):
-                    product(tile[:, j, :], w3_dealt, w3_scale, 0, b * per_bank + j, z_words[:], z_scales[:])
-                acc[n, b] = tile
+            for bank, first, last in banks:
+                tile = psum.tile([P, last - first, hi - lo], F32, name=f"acc{n}_{first}", tag=f"bank{bank}")
+                for t in range(first, last):
+                    product(tile[:, t - first, :], w3_dealt, w3_scale, 0, t, z_words[:], z_scales[:])
+                acc[n, first] = tile
 
         def scatter(t, lo, hi, values):
             nc.vector.tensor_copy(page[t][:].indirect(offsets(slot_list, lo, hi)), values)
@@ -206,13 +204,10 @@ def tile_picked_rankstep_none_po_kernel(
         nc.vector.tensor_tensor(share[0][:], rank[0][:], factor[0][:], ALU.mult)
         for i, (n, t) in enumerate(steps):
             if (n, t) == (2, 0):
-                last_product(0, (0, 1))
-                nc.scalar.copy(result[:, 1, a_lo:a_hi], acc[0, 0][:, 1, :])
-                nc.scalar.copy(result[:, 2:4, a_lo:a_hi], acc[0, 1][:])
+                last_product(0, ((0, 0, 1), (1, 1, 2), (2, 2, 4)))
             if (n, t) == (2, 3):
-                last_product(1, (2,))
-                nc.scalar.copy(result[:, 1:4, b_lo:b_hi], acc[1, 0][:, 1:4, :])
-            first_gather(n, t, {(2, 0): "z_grouped0", (2, 3): "z_grouped1"}.get((n, t)))
+                last_product(1, ((3, 0, 1), (4, 1, 4)))
+            first_gather(n, t, {(2, 0): "z_grouped0", (2, 3): "z_grouped1"}.get((n, t), f"partial{i % 3}"))
             if i + 1 < PACK:
                 nc.vector.tensor_tensor(share[i + 1][:], rank[i + 1][:], factor[i + 1][:], ALU.mult)
             if i > 0:
@@ -223,40 +218,41 @@ def tile_picked_rankstep_none_po_kernel(
         nc.scalar.copy(first_a[:], acc[0, 0][:, 0, :])
         second_gather(*steps[-1])
         group_z(2)
-        first_b = sbuf("first_b", [P, b_hi - b_lo], F32, tag="z2")
-        nc.scalar.copy(first_b[:], acc[1, 0][:, 0, :])
+        result = sbuf("result", [P, PACK, S], F32, tag="z2")
+        nc.scalar.copy(result[:, 0, b_lo:b_hi], acc[1, 0][:, 0, :])
         scatter(0, a_lo, a_hi, first_a[:])
-        last_product(2, (3,))
+        last_product(2, ((5, 0, 1), (6, 1, 4)))
         nc.scalar.copy(result[:, 0, c_lo:c_hi], acc[2, 0][:, 0, :])
-        nc.scalar.copy(result[:, 1:4, c_lo:c_hi], acc[2, 0][:, 1:4, :])
-        scatter(0, b_lo, b_hi, first_b[:])
+        nc.scalar.copy(result[:, 1, a_lo:a_hi], acc[0, 1][:, 0, :])
+        nc.scalar.copy(result[:, 1:4, b_lo:b_hi], acc[1, 1][:])
+        nc.scalar.copy(result[:, 1:4, c_lo:c_hi], acc[2, 1][:])
+        nc.scalar.copy(result[:, 2:4, a_lo:a_hi], acc[0, 2][:])
+        scatter(0, b_lo, b_hi, result[:, 0, b_lo:b_hi])
         scatter(0, c_lo, c_hi, result[:, 0, c_lo:c_hi])
 
         out_rows = out_0.rearrange("(p t) c -> p t c", t=PACK)
-        grouped = [sbuf(f"grouped{h}", [P, HALF, PACK], BF16) for h in range(2)]
+        grouped = [sbuf(f"grouped{h}", [P, hi - lo, PACK], BF16) for h, (lo, hi) in enumerate(OUT_PARTS)]
         for t in range(PACK):
             if t > 0:
                 scatter(t, 0, S, result[:, t, :])
             nc.sync.dma_start(out=out_rows[:, t, :], in_=page[t][:])
-            for h in range(2):
-                cols = slice(h * HALF, (h + 1) * HALF)
-                if t == PACK - 1 and h == 0:
-                    nc.vector.tensor_copy(grouped[h][:, :, t], page[t][:, cols])
-                elif t == PACK - 2 and h == 0:
-                    nc.scalar.copy(grouped[h][:, :, t:], page[t][:, cols].unsqueeze(2).to_broadcast([P, HALF, 2]))
+            for h, (lo, hi) in enumerate(OUT_PARTS):
+                if t == PACK - 1 and h < 2:
+                    nc.vector.tensor_copy(grouped[h][:, :, t], page[t][:, lo:hi])
+                elif t == PACK - 2 and h < 2:
+                    nc.scalar.copy(grouped[h][:, :, t:], page[t][:, lo:hi].unsqueeze(2).to_broadcast([P, hi - lo, 2]))
                 else:
-                    nc.scalar.copy(grouped[h][:, :, t], page[t][:, cols])
+                    nc.scalar.copy(grouped[h][:, :, t], page[t][:, lo:hi])
 
         out_scales = sbuf("out_scales", [P, U], U8)
-        for h in range(2):
-            cols = slice(h * HALF, (h + 1) * HALF)
-            out_words = sbuf(f"out_words{h}", [P, HALF], U32)
+        for h, (lo, hi) in enumerate(OUT_PARTS):
+            out_words = sbuf(f"out_words{h}", [P, hi - lo], U32)
             nc.vector.quantize_mx(
-                out=out_words[:].bitcast(FP8X4), scales=out_scales[:, cols], in_=grouped[h][:].rearrange("p c t -> p (c t)")
+                out=out_words[:].bitcast(FP8X4), scales=out_scales[:, lo:hi], in_=grouped[h][:].rearrange("p c t -> p (c t)")
             )
-            nc.sync.dma_start(out=words_view(out_1)[:, cols], in_=out_words[:].bitcast(I32))
+            nc.sync.dma_start(out=words_view(out_1)[:, lo:hi], in_=out_words[:].bitcast(I32))
         for q in range(4):
-            queue = nc.sync if q % 2 == 0 else nc.scalar
+            queue = nc.sync if q == 0 else nc.scalar
             queue.dma_start(
                 out=out_2[0, 4 * q : 4 * q + 4, :].bitcast(I32), in_=out_scales[32 * q : 32 * q + 4, :].bitcast(I32)
             )

@@ -122,8 +122,8 @@ def tile_picked_rankstep_none_po_kernel(
         nc.vector.tensor_copy(two_words[:], x_word_table[:].indirect(two_list[:]))
         deal_columns(nc, w12_scale[:], w12_scale_raw[:], 16)
         offs_words = sbuf("offs_words", [P, S], U32, tag="w12_scale_raw")
-        nc.vector.tensor_copy(offs_words[:], x_word_table[:].indirect(offs_list[:]))
         deal_columns(nc, w1_dealt[:].bitcast(I32), w1_raw[:].bitcast(I32), 4)
+        nc.vector.tensor_copy(offs_words[:], x_word_table[:].indirect(offs_list[:]))
         deal_columns(nc, w3_dealt[:].bitcast(I32), w3_raw[:].bitcast(I32), 4)
         deal_columns(nc, w3_scale[:], w3_scale_raw[:], 16)
 
@@ -149,12 +149,13 @@ def tile_picked_rankstep_none_po_kernel(
 
         share = [sbuf(f"share{t}", [P, S], F32) for t in range(PACK)]
         jump = [sbuf(f"jump{t}", [P, S], F32) for t in range(PACK)]
-        gate = [sbuf(f"gate{t}", [P, S], F32) for t in range(PACK)]
+        z_first = sbuf("z_first", [P, PACK, S], F32)
+        gate = [z_first[:, (t - 1) % PACK, :] for t in range(PACK)]
         factor = [sbuf(f"factor{t}", [P, S], F32) for t in range(PACK)]
         for t in range(PACK):
-            nc.scalar.activation(gate[t][:], degree[t][:], ACT.Sigmoid, bias=-math.log(5.0), scale=-1.0)
+            nc.scalar.activation(gate[t], degree[t][:], ACT.Sigmoid, bias=-math.log(5.0), scale=-1.0)
             nc.scalar.activation(
-                factor[t][:], gate[t][:], ACT.Identity, bias=factor_bias[:, t : t + 1], scale=factor_scale[:, t : t + 1]
+                factor[t][:], gate[t], ACT.Identity, bias=factor_bias[:, t : t + 1], scale=factor_scale[:, t : t + 1]
             )
             nc.scalar.activation(jump[t][:], tel_raw[t][:], ACT.Copy, scale=tel_scale[:, t : t + 1])
 
@@ -170,7 +171,7 @@ def tile_picked_rankstep_none_po_kernel(
         def second_gather(n, t):
             lo, hi = CHUNKS[n]
             if t == 0:
-                z[n] = sbuf(f"z{n}", [P, PACK, hi - lo], F32)
+                z[n] = z_first[:, :, lo:hi] if n == 0 else sbuf(f"z{n}", [P, PACK, hi - lo], F32, tag="z_first" if n == 2 else None)[:]
             nc.vector.tensor_tensor(
                 z[n][:, t, :], share[t][:].indirect(offsets(in2_list, lo, hi)), partial[n, t][:], ALU.add
             )
@@ -180,7 +181,7 @@ def tile_picked_rankstep_none_po_kernel(
             z_grouped[n] = sbuf(f"z_grouped{n}", [P, hi - lo, PACK], BF16)
             nc.scalar.copy(
                 z_grouped[n][:].rearrange("p (c i) t -> p c t i", i=4),
-                z[n][:].rearrange("p t (c i) -> p c t i", i=4),
+                z[n].rearrange("p t (c i) -> p c t i", i=4),
             )
 
         def last_product(n, banks):
@@ -200,25 +201,30 @@ def tile_picked_rankstep_none_po_kernel(
             nc.vector.tensor_copy(page[t][:].indirect(offsets(slot_list, lo, hi)), values)
 
         (a_lo, a_hi), (b_lo, b_hi), (c_lo, c_hi) = CHUNKS
-        steps = [(n, t) for n in range(len(CHUNKS)) for t in range(PACK)]
+        steps = [(n, t) for n in range(2) for t in range(PACK)]
+        waits = ("factor3", "partial0_2", "partial0_3", None)
         nc.vector.tensor_tensor(share[0][:], rank[0][:], factor[0][:], ALU.mult)
         for i, (n, t) in enumerate(steps):
-            if (n, t) == (2, 0):
-                last_product(0, ((0, 0, 1), (1, 1, 2), (2, 2, 4)))
-            if (n, t) == (2, 3):
-                last_product(1, ((3, 0, 1), (4, 1, 4)))
-            first_gather(n, t, {(2, 0): "z_grouped0", (2, 3): "z_grouped1"}.get((n, t), f"partial{i % 3}"))
+            first_gather(n, t, waits[t] if n > 0 else None)
             if i + 1 < PACK:
                 nc.vector.tensor_tensor(share[i + 1][:], rank[i + 1][:], factor[i + 1][:], ALU.mult)
             if i > 0:
                 second_gather(*steps[i - 1])
                 if t == 0:
-                    group_z(n - 1)
-        first_a = sbuf("first_a", [P, a_hi - a_lo], F32, tag="jump3")
-        nc.scalar.copy(first_a[:], acc[0, 0][:, 0, :])
+                    group_z(0)
+        first_gather(2, 0, waits[0])
         second_gather(*steps[-1])
+        group_z(1)
+        for t in range(1, PACK):
+            first_gather(2, t, waits[t])
+        last_product(0, ((0, 0, 1), (1, 1, 2), (2, 2, 4)))
+        first_a = sbuf("first_a", [P, a_hi - a_lo], F32)
+        nc.scalar.copy(first_a[:], acc[0, 0][:, 0, :])
+        for t in range(PACK):
+            second_gather(2, t)
+        last_product(1, ((3, 0, 1), (4, 1, 4)))
         group_z(2)
-        result = sbuf("result", [P, PACK, S], F32, tag="z2")
+        result = sbuf("result", [P, PACK, S], F32, tag="z_first")
         nc.scalar.copy(result[:, 0, b_lo:b_hi], acc[1, 0][:, 0, :])
         scatter(0, a_lo, a_hi, first_a[:])
         last_product(2, ((5, 0, 1), (6, 1, 4)))

import math
from contextlib import ExitStack

import concourse.mybir as mybir

F32 = mybir.dt.float32
BF16 = mybir.dt.bfloat16
I32 = mybir.dt.int32
U32 = mybir.dt.uint32
U16 = mybir.dt.uint16
U8 = mybir.dt.uint8
FP8X4 = mybir.dt.float8_e4m3fn_x4
ACT = mybir.ActivationFunctionType
ALU = mybir.AluOpType

P = 128
PACK = 4
T, S, U = 2048, 512, 1024
FEATURES = P * PACK
CHUNKS = ((0, 256), (256, 384), (384, 512))
OUT_PARTS = ((0, 256), (256, 512), (512, 768), (768, 1024))

FLOPS = 3 * 2 * FEATURES * FEATURES * S


def offsets(lists, lo, hi):
    return lists[:, lo // 16 : hi // 16]


def words_view(words):
    return words[0].rearrange("p n t -> p (n t)").bitcast(I32)


def load_scale_rows(queues, tile, first, scales):
    for q, queue in enumerate(queues):
        row = 32 * q + first
        queue.dma_start(out=tile[row : row + 4, :].bitcast(I32), in_=scales[0, 4 * q : 4 * q + 4, :].bitcast(I32))


def deal_columns(nc, dealt, raw, run):
    nc.vector.tensor_copy(
        out=dealt.rearrange("p (t c i) -> p c t i", t=PACK, i=run),
        in_=raw.rearrange("p (c i t) -> p c t i", t=PACK, i=run),
    )


def tile_picked_rankstep_none_po_kernel(
    tc, x_words, x_scales, w1_words, w1_scales, w2_words, w2_scales, tel, gn, w3_words, w3_scales, mem,
    offs, two, in1, in2, slot, out_0, out_1, out_2,
):
    nc = tc.nc
    with ExitStack() as ctx:
        keep = ctx.enter_context(tc.tile_pool(name="keep", bufs=1))
        psum = ctx.enter_context(tc.psum_pool(name="psum", bufs=1))

        def sbuf(name, shape, dtype, tag=None):
            return keep.tile(shape, dtype, name=name, tag=tag or name, align_bytes=64)

        def load_list(name, lists):
            tile = keep.tile([P, S // 16], U16, name=name)
            nc.sync.dma_start(tile[:], lists)
            return tile

        def load_words(name, words, width):
            tile = sbuf(name, [P, width], U32)
            nc.sync.dma_start(out=tile[:].bitcast(I32), in_=words_view(words))
            return tile

        x_scale_table = sbuf("x_scale_table", [P, T], U8)
        w12_scale_raw = sbuf("w12_scale_raw", [P, FEATURES], U8)
        w3_scale_raw = sbuf("w3_scale_raw", [P, FEATURES], U8)
        nc.vector.memset(w12_scale_raw[:].bitcast(I32), 0)
        nc.vector.memset(w3_scale_raw[:].bitcast(I32), 0)

        two_list = load_list("two_list", two)
        for q in range(4):
            (nc.sync if q < 2 else nc.scalar).dma_start(
                out=x_scale_table[32 * q : 32 * q + 32, :].bitcast(I32),
                in_=x_scales[0, 4 * q : 4 * q + 4, :].bitcast(I32).unsqueeze(0).to_broadcast([8, 4, T // 4]),
            )
        offs_list = load_list("offs_list", offs)
        w2_raw = load_words("w2_raw", w2_words, FEATURES)
        x_word_table = load_words("x_word_table", x_words, T)
        load_scale_rows([nc.sync] * 4, w12_scale_raw, 0, w2_scales)
        load_scale_rows([nc.sync] * 2 + [nc.gpsimd] * 2, w12_scale_raw, 4, w1_scales)
        w1_raw = load_words("w1_raw", w1_words, FEATURES)
        gain = sbuf("gain", [P, PACK], F32)
        nc.gpsimd.dma_start(out=gain[:], in_=gn.rearrange("(p t) o -> p (t o)", t=PACK))
        w3_raw = load_words("w3_raw", w3_words, FEATURES)
        load_scale_rows([nc.sync] * 4, w3_scale_raw, 0, w3_scales)
        in1_list = load_list("in1_list", in1)
        tel_rows = tel.rearrange("(p t) j -> p t j", t=PACK)
        tel_raw = [sbuf(f"tel_raw{t}", [P, S], F32) for t in range(PACK)]
        for t in range(PACK):
            nc.sync.dma_start(out=tel_raw[t][:], in_=tel_rows[:, t, :])
            if t == 0:
                in2_list = load_list("in2_list", in2)
        slot_list = load_list("slot_list", slot)
        mem_rows = mem.rearrange("(p t) c -> p t c", t=PACK)
        page = [sbuf(f"page{t}", [P, U], F32) for t in range(PACK)]
        for t in range(PACK):
            nc.sync.dma_start(out=page[t][:], in_=mem_rows[:, t, :])

        factor_scale = sbuf("factor_scale", [P, PACK], F32)
        factor_bias = sbuf("factor_bias", [P, PACK], F32)
        tel_scale = sbuf("tel_scale", [P, PACK], F32)
        nc.gpsimd.tensor_scalar(factor_scale[:], gain[:], 1.6, 0.0, ALU.mult, ALU.add)
        nc.gpsimd.tensor_scalar(factor_bias[:], gain[:], 0.4, 0.0, ALU.mult, ALU.add)
        nc.gpsimd.tensor_scalar(tel_scale[:], gain[:], 0.5, 0.0, ALU.mult, ALU.add)

        two_scales = sbuf("two_scales", [P, S], U8)
        offs_scales = sbuf("offs_scales", [P, S], U8)
        two_words = sbuf("two_words", [P, S], U32)
        w12_scale = sbuf("w12_scale", [P, FEATURES], U8)
        w3_scale = sbuf("w3_scale", [P, FEATURES], U8)
        w1_dealt = sbuf("w1_dealt", [P, FEATURES], U32)
        w2_dealt = sbuf("w2_dealt", [P, FEATURES], U32)
        w3_dealt = sbuf("w3_dealt", [P, FEATURES], U32)
        nc.vector.tensor_copy(two_scales[:], x_scale_table[:].indirect(two_list[:]))
        nc.vector.tensor_copy(offs_scales[:], x_scale_table[:].indirect(offs_list[:]))
        deal_columns(nc, w2_dealt[:].bitcast(I32), w2_raw[:].bitcast(I32), 4)
        nc.vector.tensor_copy(two_words[:], x_word_table[:].indirect(two_list[:]))
        deal_columns(nc, w12_scale[:], w12_scale_raw[:], 16)
        offs_words = sbuf("offs_words", [P, S], U32, tag="w12_scale_raw")
        deal_columns(nc, w1_dealt[:].bitcast(I32), w1_raw[:].bitcast(I32), 4)
        nc.vector.tensor_copy(offs_words[:], x_word_table[:].indirect(offs_list[:]))
        deal_columns(nc, w3_dealt[:].bitcast(I32), w3_raw[:].bitcast(I32), 4)
        deal_columns(nc, w3_scale[:], w3_scale_raw[:], 16)

        def product(out, weights, weight_scales, first, t, moving, moving_scales):
            cols = slice(t * P, (t + 1) * P)
            nc.tensor.matmul_mx(
                out=out,
                lhsT=weights[:, cols].bitcast(FP8X4),
                lhsT_scale=weight_scales[first:P, cols],
                rhs=moving.bitcast(FP8X4),
                rhs_scale=moving_scales,
                start=True,
                stop=True,
            )

        degree = [psum.tile([P, S], F32, name=f"degree{t}", tag=f"bank{t}") for t in range(PACK)]
        rank = [psum.tile([P, S], F32, name=f"rank{t}", tag=f"bank{PACK + t}") for t in range(PACK)]
        product(degree[0][:], w2_dealt, w12_scale, 0, 0, two_words[:], two_scales[:])
        for t in range(PACK):
            if t + 1 < PACK:
                product(degree[t + 1][:], w2_dealt, w12_scale, 0, t + 1, two_words[:], two_scales[:])
            product(rank[t][:], w1_dealt, w12_scale, 4, t, offs_words[:], offs_scales[:])

        share = [sbuf(f"share{t}", [P, S], F32) for t in range(PACK)]
        jump = [sbuf(f"jump{t}", [P, S], F32) for t in range(PACK)]
        z_first = sbuf("z_first", [P, PACK, S], F32)
        gate = [z_first[:, (t - 1) % PACK, :] for t in range(PACK)]
        factor = [sbuf(f"factor{t}", [P, S], F32) for t in range(PACK)]
        for t in range(PACK):
            nc.scalar.activation(gate[t], degree[t][:], ACT.Sigmoid, bias=-math.log(5.0), scale=-1.0)
            nc.scalar.activation(
                factor[t][:], gate[t], ACT.Identity, bias=factor_bias[:, t : t + 1], scale=factor_scale[:, t : t + 1]
            )
            nc.scalar.activation(jump[t][:], tel_raw[t][:], ACT.Copy, scale=tel_scale[:, t : t + 1])

        partial, z, z_grouped, acc = {}, {}, {}, {}

        def first_gather(n, t, tag=None):
            lo, hi = CHUNKS[n]
            partial[n, t] = sbuf(f"partial{n}_{t}", [P, hi - lo], F32, tag=tag)
            nc.vector.tensor_tensor(
                partial[n, t][:], share[t][:].indirect(offsets(in1_list, lo, hi)), jump[t][:, lo:hi], ALU.add
            )

        def second_gather(n, t):
            lo, hi = CHUNKS[n]
            if t == 0:
                z[n] = z_first[:, :, lo:hi] if n == 0 else sbuf(f"z{n}", [P, PACK, hi - lo], F32, tag="z_first" if n == 2 else None)[:]
            nc.vector.tensor_tensor(
                z[n][:, t, :], share[t][:].indirect(offsets(in2_list, lo, hi)), partial[n, t][:], ALU.add
            )

        def group_z(n):
            lo, hi = CHUNKS[n]
            z_grouped[n] = sbuf(f"z_grouped{n}", [P, hi - lo, PACK], BF16)
            nc.scalar.copy(
                z_grouped[n][:].rearrange("p (c i) t -> p c t i", i=4),
                z[n].rearrange("p t (c i) -> p c t i", i=4),
            )

        def last_product(n, banks):
            lo, hi = CHUNKS[n]
            z_words = sbuf(f"z_words{n}", [P, hi - lo], U32)
            z_scales = sbuf(f"z_scales{n}", [P, hi - lo], U8)
            nc.vector.quantize_mx(
                out=z_words[:].bitcast(FP8X4), scales=z_scales[:], in_=z_grouped[n][:].rearrange("p c t -> p (c t)")
            )
            for bank, first, last in banks:
                tile = psum.tile([P, last - first, hi - lo], F32, name=f"acc{n}_{first}", tag=f"bank{bank}")
                for t in range(first, last):
                    product(tile[:, t - first, :], w3_dealt, w3_scale, 0, t, z_words[:], z_scales[:])
                acc[n, first] = tile

        def scatter(t, lo, hi, values):
            nc.vector.tensor_copy(page[t][:].indirect(offsets(slot_list, lo, hi)), values)

        (a_lo, a_hi), (b_lo, b_hi), (c_lo, c_hi) = CHUNKS
        steps = [(n, t) for n in range(2) for t in range(PACK)]
        waits = ("factor3", "partial0_2", "partial0_3", None)
        nc.vector.tensor_tensor(share[0][:], rank[0][:], factor[0][:], ALU.mult)
        for i, (n, t) in enumerate(steps):
            first_gather(n, t, waits[t] if n > 0 else None)
            if i + 1 < PACK:
                nc.vector.tensor_tensor(share[i + 1][:], rank[i + 1][:], factor[i + 1][:], ALU.mult)
            if i > 0:
                second_gather(*steps[i - 1])
                if t == 0:
                    group_z(0)
        first_gather(2, 0, waits[0])
        second_gather(*steps[-1])
        group_z(1)
        for t in range(1, PACK):
            first_gather(2, t, waits[t])
        last_product(0, ((0, 0, 1), (1, 1, 2), (2, 2, 4)))
        first_a = sbuf("first_a", [P, a_hi - a_lo], F32)
        nc.scalar.copy(first_a[:], acc[0, 0][:, 0, :])
        for t in range(PACK):
            second_gather(2, t)
        last_product(1, ((3, 0, 1), (4, 1, 4)))
        group_z(2)
        result = sbuf("result", [P, PACK, S], F32, tag="z_first")
        nc.scalar.copy(result[:, 0, b_lo:b_hi], acc[1, 0][:, 0, :])
        scatter(0, a_lo, a_hi, first_a[:])
        last_product(2, ((5, 0, 1), (6, 1, 4)))
        nc.scalar.copy(result[:, 0, c_lo:c_hi], acc[2, 0][:, 0, :])
        nc.scalar.copy(result[:, 1, a_lo:a_hi], acc[0, 1][:, 0, :])
        nc.scalar.copy(result[:, 1:4, b_lo:b_hi], acc[1, 1][:])
        nc.scalar.copy(result[:, 1:4, c_lo:c_hi], acc[2, 1][:])
        nc.scalar.copy(result[:, 2:4, a_lo:a_hi], acc[0, 2][:])
        scatter(0, b_lo, b_hi, result[:, 0, b_lo:b_hi])
        scatter(0, c_lo, c_hi, result[:, 0, c_lo:c_hi])

        out_rows = out_0.rearrange("(p t) c -> p t c", t=PACK)
        grouped = [sbuf(f"grouped{h}", [P, hi - lo, PACK], BF16) for h, (lo, hi) in enumerate(OUT_PARTS)]
        for t in range(PACK):
            if t > 0:
                scatter(t, 0, S, result[:, t, :])
            nc.sync.dma_start(out=out_rows[:, t, :], in_=page[t][:])
            for h, (lo, hi) in enumerate(OUT_PARTS):
                if t == PACK - 1 and h < 2:
                    nc.vector.tensor_copy(grouped[h][:, :, t], page[t][:, lo:hi])
                elif t == PACK - 2 and h < 2:
                    nc.scalar.copy(grouped[h][:, :, t:], page[t][:, lo:hi].unsqueeze(2).to_broadcast([P, hi - lo, 2]))
                else:
                    nc.scalar.copy(grouped[h][:, :, t], page[t][:, lo:hi])

        out_scales = sbuf("out_scales", [P, U], U8)
        for h, (lo, hi) in enumerate(OUT_PARTS):
            out_words = sbuf(f"out_words{h}", [P, hi - lo], U32)
            nc.vector.quantize_mx(
                out=out_words[:].bitcast(FP8X4), scales=out_scales[:, lo:hi], in_=grouped[h][:].rearrange("p c t -> p (c t)")
            )
            nc.sync.dma_start(out=words_view(out_1)[:, lo:hi], in_=out_words[:].bitcast(I32))
        for q in range(4):
            queue = nc.sync if q == 0 else nc.scalar
            queue.dma_start(
                out=out_2[0, 4 * q : 4 * q + 4, :].bitcast(I32), in_=out_scales[32 * q : 32 * q + 4, :].bitcast(I32)
            )
